import numpy as np
import ml_dtypes


def mxq(x, axis, fmt="e4m3"):
    dtype, down = {"e4m3": (ml_dtypes.float8_e4m3fn, 7), "e5m2": (ml_dtypes.float8_e5m2, 14)}[fmt]
    v = np.moveaxis(np.asarray(x, np.float32).astype(ml_dtypes.bfloat16).astype(np.float64), axis, -1)
    blocks = v.reshape(v.shape[:-1] + (-1, 32))
    amax = np.abs(blocks).max(-1, keepdims=True)
    byte = np.maximum(np.where(amax > 0, np.frexp(amax)[1] - 1 + 127, 0) - down, 1)
    scale = np.exp2(byte - 127.0)
    codes = (blocks / scale).astype(np.float32).astype(dtype).astype(np.float64)
    return np.moveaxis((codes * scale).reshape(v.shape), -1, axis)


WIDE = False


def mx_kscale(k):
    if not WIDE:
        return np.ones(k)
    levels = np.array([10, -10, 5, -5, 0])
    if k % 512:
        return np.exp2(np.random.permutation(np.resize(levels, k // 32))).repeat(32)
    a = np.empty((k // 512, 16))
    for p in range(k // 512):
        a[p, :8] = np.random.permutation(np.resize(levels, 8))
        for g in range(8):
            far = levels[np.abs(levels - a[p, g]) >= 10]
            a[p, g + 8] = far[np.random.randint(len(far))]
    return np.exp2(a.ravel()).repeat(32)


def f64(x):
    return np.asarray(x).astype(np.float64)


def striped(idx):
    return np.tile(np.asarray(idx).reshape(-1, 16).T, (8, 1)).astype(np.uint16)


def unstriped(offs):
    return offs[:16].T.reshape(-1).astype(np.int64)


def striped8(idx):
    return np.asarray(idx).reshape(8, -1, 16).transpose(0, 2, 1).reshape(128, -1).astype(np.uint16)


def unstriped8(offs):
    return offs.reshape(8, 16, -1).transpose(0, 2, 1).reshape(8, -1).astype(np.int64)


def pick8(x, idx, run):
    r = np.arange(len(x))
    return x[r[:, None], idx[r % (8 * run) // run]]


E2M1 = np.array([0.0, 0.5, 1.0, 1.5, 2.0, 3.0, 4.0, 6.0, -0.0, -0.5, -1.0, -1.5, -2.0, -3.0, -4.0, -6.0])


def pack_weight(w, fmt):
    k, n = w.shape
    w = f64(np.asarray(w, np.float32).astype(ml_dtypes.bfloat16)).reshape(k // 32, 32, n)
    amax = np.abs(w).max(1)
    if fmt == "e4m3":
        byte = np.frexp(amax)[1] - 1 + 127 - 7
    else:
        mant, ex = np.frexp(amax / 6.0)
        byte = np.where(mant > 0.5, ex, ex - 1) + 127
    byte = np.clip(np.where(amax > 0, byte, 1), 1, 254)
    scaled = (w * np.exp2(127.0 - byte)[:, None, :]).reshape(k, n).astype(np.float32)
    by_word = np.ascontiguousarray(scaled.reshape(k // 512, 128, 4, n).transpose(0, 1, 3, 2))
    if fmt == "e4m3":
        words = by_word.astype(ml_dtypes.float8_e4m3fn).view(np.uint8)
    else:
        c = by_word.astype(ml_dtypes.float4_e2m1fn).view(np.uint8) & 0xF
        words = (c[..., 0::2] | (c[..., 1::2] << 4)).reshape(k // 512, 128, 2 * n)
    return np.ascontiguousarray(words), np.ascontiguousarray(byte.astype(np.uint8).reshape(k // 512, 16, n))


def unpack_weight(words, scales, fmt):
    g, _, n = scales.shape
    words = np.ascontiguousarray(words).reshape(g, 128, n, -1)
    if fmt == "e4m3":
        vals = words.view(ml_dtypes.float8_e4m3fn).astype(np.float64)
    else:
        nib = np.empty((g, 128, n, 4), np.uint8)
        nib[..., 0::2] = words & 0xF
        nib[..., 1::2] = words >> 4
        vals = E2M1[nib]
    vals = vals * np.repeat(np.exp2(scales.astype(np.float64) - 127.0), 8, axis=1)[..., None]
    return vals.transpose(0, 1, 3, 2).reshape(g * 512, n)


K, J, R, T, Z, M, C, D, N, S = 512, 384, 512, 2048, 512, 1024, 512, 1024, 256, 1024


def setup_inputs():
    n = np.random.standard_normal
    idx = np.random.permutation(T)[:J]
    idx2 = np.random.permutation(M)[:J]
    idx3 = np.stack([np.random.permutation(C)[:J] for _ in range(8)])
    idx4 = np.stack([np.random.permutation(D)[:C] for _ in range(8)])
    idx5 = np.random.permutation(S)[:N]
    fk = mx_kscale(K)
    fr = mx_kscale(R)
    fz = mx_kscale(Z)
    xtp = pack_weight(n((K, T)) * fk[:, None], "e4m3")
    wp = pack_weight(n((K, R)) * 1 / np.sqrt(K) / fk[:, None] * fr, "e2m1")
    xop = pack_weight(n((Z, M)) / fz[:, None], "e2m1")
    w2p = pack_weight(n((Z, R)) * 1 / np.sqrt(Z) * fz[:, None] * fr, "e4m3")
    vsp = pack_weight(n((R, S)) * 1 / np.sqrt(R) / fr[:, None], "e4m3")
    return {
        "xt_words": xtp[0],
        "xt_scales": xtp[1],
        "w_words": wp[0],
        "w_scales": wp[1],
        "xo_words": xop[0],
        "xo_scales": xop[1],
        "w2_words": w2p[0],
        "w2_scales": w2p[1],
        "tl": (np.random.randint(1, 9, (R, D)).astype(np.float64)).astype(np.float32),
        "sl": ((np.random.randint(4, 13, (R, 1)) / 64.0) * fr[:, None]).astype(np.float32),
        "vs_words": vsp[0],
        "vs_scales": vsp[1],
        "offs": striped(idx),
        "offs2": striped(idx2),
        "offs3": striped8(idx3),
        "offs4": striped8(idx4),
        "offs5": striped(idx5),
    }


def reference(xt_words, xt_scales, w_words, w_scales, xo_words, xo_scales, w2_words, w2_scales, tl, sl, vs_words, vs_scales, offs, offs2, offs3, offs4, offs5):
    idx = unstriped(offs)
    idx2 = unstriped(offs2)
    idx3 = unstriped8(offs3)
    idx4 = unstriped8(offs4)
    idx5 = unstriped(offs5)
    xtu = unpack_weight(xt_words, xt_scales, "e4m3")
    wu = unpack_weight(w_words, w_scales, "e2m1")
    xou = unpack_weight(xo_words, xo_scales, "e2m1")
    w2u = unpack_weight(w2_words, w2_scales, "e4m3")
    vsu = unpack_weight(vs_words, vs_scales, "e4m3")
    xtidxg = xtu[:, idx]
    xoidx2g = xou[:, idx2]
    a = wu.T @ xtidxg + w2u.T @ xoidx2g
    pw = np.zeros((R, C))
    pw[np.arange(R)[:, None], idx3[np.arange(R) % 512 // 64]] = a
    hid = np.maximum(np.abs(pw) - pick8(f64(tl), idx4, 64) * f64(sl), 0.0)
    vsidx5g = vsu[:, idx5]
    hidq = mxq(hid, 0, "e4m3")
    y = vsidx5g.T @ hidq
    return y

@@ -1,0 +1,221 @@
+from contextlib import ExitStack
+
+import concourse.mybir as mybir
+
+F32 = mybir.dt.float32
+BF16 = mybir.dt.bfloat16
+I32 = mybir.dt.int32
+U32 = mybir.dt.uint32
+U16 = mybir.dt.uint16
+U8 = mybir.dt.uint8
+FP8X4 = mybir.dt.float8_e4m3fn_x4
+FP4X4 = mybir.dt.float4_e2m1fn_x4
+ALU = mybir.AluOpType
+COPY = mybir.ActivationFunctionType.Copy
+
+P = 128
+PACK = 4
+QUADS = 4
+K, J, R, T, Z, M, C, D, N, S = 512, 384, 512, 2048, 512, 1024, 512, 1024, 256, 1024
+HALF = C // 2
+SLOT_PIECES = ((0, 256), (256, 384))
+
+FLOPS = 2 * K * R * J + 2 * Z * R * J + 2 * R * N * C
+
+
+def tile_picked_tokens_plain_bank_shrunk_store_plain_kernel(
+    tc, xt_words, xt_scales, w_words, w_scales, xo_words, xo_scales, w2_words, w2_scales, tl, sl,
+    vs_words, vs_scales, offs, offs2, offs3, offs4, offs5, out,
+):
+    nc = tc.nc
+    with ExitStack() as ctx:
+        lists = ctx.enter_context(tc.tile_pool(name="lists", bufs=1))
+        sb = ctx.enter_context(tc.tile_pool(name="sb", bufs=1))
+        ps = ctx.enter_context(tc.psum_pool(name="ps", bufs=1))
+
+        def tile(shape, dtype, name, tag=None):
+            return sb.tile(shape, dtype, name=name, tag=tag or name, align_bytes=64)
+
+        def load_list(src, name):
+            dst = lists.tile([P, src.shape[1]], U16, name=name)
+            nc.sync.dma_start(dst[:], src)
+            return dst
+
+        def load_scale_rows(queue, dst, src):
+            for q in range(QUADS):
+                queue.dma_start(out=dst[32 * q : 32 * q + 4, :].bitcast(I32), in_=src[0, 4 * q : 4 * q + 4, :].bitcast(I32))
+
+        def words8(src):
+            return src[0].rearrange("p c b -> p (c b)").bitcast(I32)
+
+        xo_sc = tile([P, M], U8, "xo_sc")
+        xt_sc = tile([P, T], U8, "xt_sc")
+        vs_sc = tile([P, S], U8, "vs_sc")
+        wst = tile([4, QUADS, 2 * R], U8, "wst")
+        wsc = tile([P, 2 * R], U8, "wsc")
+        boards = [tile([P, C], F32, "board%d" % t) for t in range(PACK)]
+        nc.vector.memset(xo_sc[:].bitcast(I32), 0)
+        nc.vector.memset(xt_sc[:].bitcast(I32), 0)
+        nc.vector.memset(wsc[:].bitcast(I32), 0)
+        nc.vector.memset(vs_sc[:].bitcast(I32), 0)
+        for t in range(PACK):
+            nc.vector.memset(boards[t][:], 0.0)
+
+        steps = tile([P, PACK], F32, "steps")
+
+        def stage_scales(queue, dst, src):
+            queue.dma_start(
+                out=dst.bitcast(I32),
+                in_=src[0].bitcast(I32).rearrange("(q i) c -> i q c", q=QUADS),
+            )
+
+        levels = [tile([P, D], F32, "levels%d" % t) for t in range(PACK)]
+        tl_rows = tl.rearrange("(p t) d -> t p d", t=PACK)
+        xt_w = tile([P, T], U32, "xt_w")
+        xo_w = tile([P, M], U16, "xo_w")
+        vs_w = tile([P, S], U32, "vs_w")
+        w_w = tile([P, R], U16, "w_w")
+        w2_w = tile([P, R], U32, "w2_w")
+
+        nc.gpsimd.dma_start(out=steps[:], in_=sl.rearrange("(p t) o -> p (t o)", t=PACK))
+        l2 = load_list(offs2, "l2")
+        stage_scales(nc.sync, wst[:, :, 0:R], w_scales)
+        stage_scales(nc.sync, wst[:, :, R : 2 * R], w2_scales)
+        load_scale_rows(nc.sync, xo_sc, xo_scales)
+        nc.sync.dma_start(out=xt_w[:].bitcast(I32), in_=words8(xt_words))
+        l1 = load_list(offs, "l1")
+        load_scale_rows(nc.sync, xt_sc, xt_scales)
+        nc.sync.dma_start(out=w_w[:].bitcast(I32), in_=w_words[0].bitcast(I32))
+        nc.sync.dma_start(out=xo_w[:].bitcast(I32), in_=xo_words[0].bitcast(I32))
+        nc.sync.dma_start(out=w2_w[:].bitcast(I32), in_=words8(w2_words))
+        l4 = load_list(offs4, "l4")
+        nc.sync.dma_start(out=levels[0][:], in_=tl_rows[0])
+        l3 = load_list(offs3, "l3")
+        for t in range(1, PACK):
+            nc.sync.dma_start(out=levels[t][:], in_=tl_rows[t])
+        nc.sync.dma_start(out=vs_w[:].bitcast(I32), in_=words8(vs_words))
+        l5 = load_list(offs5, "l5")
+        load_scale_rows(nc.sync, vs_sc, vs_scales)
+
+        cuts = [tile([P, C], F32, "cut%d" % t) for t in range(PACK - 1)]
+
+        def fetch_levels(dst, t, c0, c1):
+            nc.scalar.activation(
+                out=dst, in_=levels[t][:].indirect(l4[:, c0 // 16 : c1 // 16]), func=COPY, scale=steps[:, t : t + 1]
+            )
+
+        xo_gs = tile([P, J], U8, "xo_gs")
+        xo_gw = tile([P, J], U16, "xo_gw")
+        xt_gs = tile([P, J], U8, "xt_gs")
+        xt_gw = tile([P, J], U32, "xt_gw")
+        wds = tile([P, 2, R], U8, "wds")
+        w_dw = tile([P, R], U16, "w_dw")
+        w2_dw = tile([P, R], U32, "w2_dw")
+
+        def dealt(ap):
+            return ap.rearrange("p (t m) -> p t m", t=PACK)
+
+        def undealt(ap):
+            return ap.rearrange("p (m t) -> p t m", t=PACK)
+
+        for q in range(QUADS):
+            nc.vector.tensor_copy(wsc[32 * q : 32 * q + 4, :].bitcast(I32), wst[:, q, :].bitcast(I32))
+        nc.vector.tensor_copy(xo_gs[:], xo_sc[:].indirect(l2[:]))
+        nc.vector.tensor_copy(
+            wds[:].rearrange("p w (t m) -> p w t m", t=PACK), wsc[:].rearrange("p (w m t) -> p w t m", w=2, t=PACK)
+        )
+        nc.vector.tensor_copy(xt_gw[:], xt_w[:].indirect(l1[:]))
+        nc.scalar.copy(dealt(w_dw[:]), undealt(w_w[:]))
+        nc.scalar.copy(dealt(w2_dw[:]), undealt(w2_w[:]))
+        nc.vector.tensor_copy(xt_gs[:], xt_sc[:].indirect(l1[:]))
+        nc.vector.tensor_copy(xo_gw[:], xo_w[:].indirect(l2[:]))
+
+        accs = [ps.tile([P, C], F32, name="acc%d" % t) for t in range(PACK)]
+        for t in range(PACK):
+            cols = slice(t * P, (t + 1) * P)
+            for i, (j0, j1) in enumerate(SLOT_PIECES):
+                nc.tensor.matmul_mx(
+                    out=accs[t][:, j0:j1], lhsT=w_dw[:, cols].bitcast(FP4X4), lhsT_scale=wds[:, 0, cols],
+                    rhs=xt_gw[:, j0:j1].bitcast(FP8X4), rhs_scale=xt_gs[:, j0:j1], start=(i == 0), stop=False,
+                )
+            for i, (j0, j1) in enumerate(SLOT_PIECES):
+                nc.tensor.matmul_mx(
+                    out=accs[t][:, j0:j1], lhsT=w2_dw[:, cols].bitcast(FP8X4), lhsT_scale=wds[:, 1, cols],
+                    rhs=xo_gw[:, j0:j1].bitcast(FP4X4), rhs_scale=xo_gs[:, j0:j1],
+                    start=False, stop=(i == len(SLOT_PIECES) - 1),
+                )
+
+        def put(t, src):
+            nc.vector.tensor_copy(src, accs[t][:, 0:J])
+            nc.scalar.activation(out=boards[t][:].indirect(l3[:]), in_=src, func=COPY)
+
+        fetch_levels(cuts[0][:], 0, 0, C)
+        put(0, tile([P, J], F32, "hidden0")[:])
+        fetch_levels(cuts[1][:], 1, 0, C)
+        put(1, tile([P, J], F32, "hidden1")[:])
+        fetch_levels(cuts[2][:], 2, 0, C)
+        put(2, tile([P, J], F32, "hidden2", tag="levels1")[:])
+        last = tile([P, C], F32, "last", tag="levels2")
+        put(3, last[:, 64 : 64 + J])
+        for h in range(2):
+            fetch_levels(last[:, h * HALF : (h + 1) * HALF], 3, h * HALF, (h + 1) * HALF)
+        cut = [c[:] for c in cuts] + [last[:]]
+
+        vs_gs = tile([P, N], U8, "vs_gs")
+        vs_gw = tile([P, N], U32, "vs_gw")
+
+        halves = [slice(h * HALF, (h + 1) * HALF) for h in range(2)]
+        mags = [tile([P, C], F32, "mags%d" % t) for t in range(2)]
+        early = tile([P, 2 * C], F32, "early")
+        hid = [tile([P, HALF * PACK], BF16, "hid%d" % h) for h in range(2)]
+        codes = tile([P, C], U32, "codes")
+        planes = tile([P, C], U8, "planes")
+
+        def magnitude(t, cs):
+            nc.vector.scalar_tensor_tensor(
+                out=mags[t][:, cs], in0=boards[t][:, cs], scalar=-1.0, in1=boards[t][:, cs], op0=ALU.mult, op1=ALU.max
+            )
+
+        def take_off(dst, t, cs):
+            nc.vector.tensor_tensor(dst, mags[t][:, cs], cut[t][:, cs], ALU.subtract)
+
+        def keep_positive(h, t0, pair):
+            nc.vector.tensor_scalar(
+                out=hid[h][:].rearrange("p (c t) -> p c t", t=PACK)[:, :, t0 : t0 + 2], in0=pair,
+                scalar1=0.0, scalar2=None, op0=ALU.max,
+            )
+
+        whole = slice(0, C)
+        for t in range(2):
+            magnitude(t, whole)
+            take_off(early[:, t * C : (t + 1) * C], t, whole)
+        nc.vector.tensor_copy(vs_gs[:], vs_sc[:].indirect(l5[:]))
+        nc.vector.tensor_copy(vs_gw[:], vs_w[:].indirect(l5[:]))
+        for h, cs in enumerate(halves):
+            keep_positive(h, 0, early[:].rearrange("p (t c) -> p c t", t=2)[:, cs, :])
+        mags.append(tile([P, C], F32, "mags2", tag="vs_w"))
+        mags.append(mags[2])
+        late = [tile([P, 2 * HALF], F32, "late0", tag="vs_sc"), tile([P, 2 * HALF], F32, "late1")]
+        magnitude(2, whole)
+        for h, cs in enumerate(halves):
+            take_off(late[h][:, 0:HALF], 2, cs)
+        for cs in halves:
+            magnitude(3, cs)
+        out_rows = out.rearrange("(u p) c -> p u c", p=P)
+        for h, cs in enumerate(halves):
+            take_off(late[h][:, HALF : 2 * HALF], 3, cs)
+            keep_positive(h, 2, late[h][:].rearrange("p (t c) -> p c t", t=2))
+            nc.vector.quantize_mx(out=codes[:, cs].bitcast(FP8X4), scales=planes[:, cs], in_=hid[h][:])
+            res = tile([P, N // P, HALF], F32, "res%d" % h)
+            for u in range(N // P):
+                rows = slice(u * P, (u + 1) * P)
+                y = ps.tile([P, HALF], F32, name="y%d%d" % (h, u))
+                nc.tensor.matmul_mx(
+                    out=y[:], lhsT=vs_gw[:, rows].bitcast(FP8X4), lhsT_scale=vs_gs[:, rows],
+                    rhs=codes[:, cs].bitcast(FP8X4), rhs_scale=planes[:, cs], start=True, stop=True,
+                )
+                if h == 1 and u == 1:
+                    nc.vector.tensor_copy(res[:, u, :], y[:])
+                else:
+                    nc.scalar.copy(res[:, u, :], y[:])
+            nc.sync.dma_start(out=out_rows[:, :, cs], in_=res[:])

@@ -53,10 +53,11 @@ def tile_picked_tokens_plain_bank_shrunk_store_plain_kernel(
         vs_sc = tile([P, S], U8, "vs_sc")
         wst = tile([4, QUADS, 2 * R], U8, "wst")
         wsc = tile([P, 2 * R], U8, "wsc")
+        xo_st = tile([4, QUADS, M], U8, "xo_st")
         boards = [tile([P, C], F32, "board%d" % t) for t in range(PACK)]
+        nc.vector.memset(wsc[:].bitcast(I32), 0)
         nc.vector.memset(xo_sc[:].bitcast(I32), 0)
         nc.vector.memset(xt_sc[:].bitcast(I32), 0)
-        nc.vector.memset(wsc[:].bitcast(I32), 0)
         nc.vector.memset(vs_sc[:].bitcast(I32), 0)
         for t in range(PACK):
             nc.vector.memset(boards[t][:], 0.0)
@@ -77,25 +78,25 @@ def tile_picked_tokens_plain_bank_shrunk_store_plain_kernel(
         w_w = tile([P, R], U16, "w_w")
         w2_w = tile([P, R], U32, "w2_w")
 
+        nc.gpsimd.dma_start(out=w_w[:].bitcast(I32), in_=w_words[0].bitcast(I32))
         nc.gpsimd.dma_start(out=steps[:], in_=sl.rearrange("(p t) o -> p (t o)", t=PACK))
-        l2 = load_list(offs2, "l2")
         stage_scales(nc.sync, wst[:, :, 0:R], w_scales)
         stage_scales(nc.sync, wst[:, :, R : 2 * R], w2_scales)
-        load_scale_rows(nc.sync, xo_sc, xo_scales)
-        nc.sync.dma_start(out=xt_w[:].bitcast(I32), in_=words8(xt_words))
-        l1 = load_list(offs, "l1")
-        load_scale_rows(nc.sync, xt_sc, xt_scales)
-        nc.sync.dma_start(out=w_w[:].bitcast(I32), in_=w_words[0].bitcast(I32))
+        l2 = load_list(offs2, "l2")
+        stage_scales(nc.sync, xo_st[:], xo_scales)
         nc.sync.dma_start(out=xo_w[:].bitcast(I32), in_=xo_words[0].bitcast(I32))
         nc.sync.dma_start(out=w2_w[:].bitcast(I32), in_=words8(w2_words))
+        l1 = load_list(offs, "l1")
+        nc.sync.dma_start(out=xt_w[:].bitcast(I32), in_=words8(xt_words))
+        load_scale_rows(nc.sync, xt_sc, xt_scales)
         l4 = load_list(offs4, "l4")
-        nc.sync.dma_start(out=levels[0][:], in_=tl_rows[0])
-        l3 = load_list(offs3, "l3")
-        for t in range(1, PACK):
+        for t in range(PACK - 1):
             nc.sync.dma_start(out=levels[t][:], in_=tl_rows[t])
-        nc.sync.dma_start(out=vs_w[:].bitcast(I32), in_=words8(vs_words))
-        l5 = load_list(offs5, "l5")
+        l3 = load_list(offs3, "l3")
+        nc.sync.dma_start(out=levels[3][:], in_=tl_rows[3])
         load_scale_rows(nc.sync, vs_sc, vs_scales)
+        l5 = load_list(offs5, "l5")
+        nc.sync.dma_start(out=vs_w[:].bitcast(I32), in_=words8(vs_words))
 
         cuts = [tile([P, C], F32, "cut%d" % t) for t in range(PACK - 1)]
 
@@ -109,7 +110,6 @@ def tile_picked_tokens_plain_bank_shrunk_store_plain_kernel(
         xt_gs = tile([P, J], U8, "xt_gs")
         xt_gw = tile([P, J], U32, "xt_gw")
         wds = tile([P, 2, R], U8, "wds")
-        w_dw = tile([P, R], U16, "w_dw")
         w2_dw = tile([P, R], U32, "w2_dw")
 
         def dealt(ap):
@@ -120,28 +120,32 @@ def tile_picked_tokens_plain_bank_shrunk_store_plain_kernel(
 
         for q in range(QUADS):
             nc.vector.tensor_copy(wsc[32 * q : 32 * q + 4, :].bitcast(I32), wst[:, q, :].bitcast(I32))
-        nc.vector.tensor_copy(xo_gs[:], xo_sc[:].indirect(l2[:]))
-        nc.vector.tensor_copy(
-            wds[:].rearrange("p w (t m) -> p w t m", t=PACK), wsc[:].rearrange("p (w m t) -> p w t m", w=2, t=PACK)
-        )
-        nc.vector.tensor_copy(xt_gw[:], xt_w[:].indirect(l1[:]))
-        nc.scalar.copy(dealt(w_dw[:]), undealt(w_w[:]))
+        for q in range(QUADS):
+            nc.vector.tensor_copy(xo_sc[32 * q : 32 * q + 4, :].bitcast(I32), xo_st[:, q, :].bitcast(I32))
+        nc.gpsimd.tensor_copy(dealt(wds[:, 1, :]), undealt(wsc[:, R : 2 * R]))
+        nc.gpsimd.tensor_copy(dealt(wds[:, 0, :]), undealt(wsc[:, 0:R]))
         nc.scalar.copy(dealt(w2_dw[:]), undealt(w2_w[:]))
-        nc.vector.tensor_copy(xt_gs[:], xt_sc[:].indirect(l1[:]))
+        w_dw = tile([P, R], U16, "w_dw", tag="w2_w")
+        nc.scalar.copy(dealt(w_dw[:]), undealt(w_w[:]))
+        nc.vector.tensor_copy(xo_gs[:], xo_sc[:].indirect(l2[:]))
         nc.vector.tensor_copy(xo_gw[:], xo_w[:].indirect(l2[:]))
+        nc.vector.tensor_copy(xt_gw[:], xt_w[:].indirect(l1[:]))
+        nc.vector.tensor_copy(xt_gs[:], xt_sc[:].indirect(l1[:]))
 
         accs = [ps.tile([P, C], F32, name="acc%d" % t) for t in range(PACK)]
         for t in range(PACK):
             cols = slice(t * P, (t + 1) * P)
             for i, (j0, j1) in enumerate(SLOT_PIECES):
                 nc.tensor.matmul_mx(
-                    out=accs[t][:, j0:j1], lhsT=w_dw[:, cols].bitcast(FP4X4), lhsT_scale=wds[:, 0, cols],
-                    rhs=xt_gw[:, j0:j1].bitcast(FP8X4), rhs_scale=xt_gs[:, j0:j1], start=(i == 0), stop=False,
+                    out=accs[t][:, j0:j1], lhsT=w2_dw[:, cols].bitcast(FP8X4), lhsT_scale=wds[:, 1, cols],
+                    rhs=xo_gw[:, j0:j1].bitcast(FP4X4), rhs_scale=xo_gs[:, j0:j1], start=(i == 0), stop=False,
                 )
+        for t in range(PACK):
+            cols = slice(t * P, (t + 1) * P)
             for i, (j0, j1) in enumerate(SLOT_PIECES):
                 nc.tensor.matmul_mx(
-                    out=accs[t][:, j0:j1], lhsT=w2_dw[:, cols].bitcast(FP8X4), lhsT_scale=wds[:, 1, cols],
-                    rhs=xo_gw[:, j0:j1].bitcast(FP4X4), rhs_scale=xo_gs[:, j0:j1],
+                    out=accs[t][:, j0:j1], lhsT=w_dw[:, cols].bitcast(FP4X4), lhsT_scale=wds[:, 0, cols],
+                    rhs=xt_gw[:, j0:j1].bitcast(FP8X4), rhs_scale=xt_gs[:, j0:j1],
                     start=False, stop=(i == len(SLOT_PIECES) - 1),
                 )
 
@@ -150,12 +154,12 @@ def tile_picked_tokens_plain_bank_shrunk_store_plain_kernel(
             nc.scalar.activation(out=boards[t][:].indirect(l3[:]), in_=src, func=COPY)
 
         fetch_levels(cuts[0][:], 0, 0, C)
-        put(0, tile([P, J], F32, "hidden0")[:])
         fetch_levels(cuts[1][:], 1, 0, C)
-        put(1, tile([P, J], F32, "hidden1")[:])
         fetch_levels(cuts[2][:], 2, 0, C)
-        put(2, tile([P, J], F32, "hidden2", tag="levels1")[:])
-        last = tile([P, C], F32, "last", tag="levels2")
+        put(0, tile([P, J], F32, "hidden0")[:])
+        put(1, tile([P, J], F32, "hidden1")[:])
+        put(2, tile([P, J], F32, "hidden2")[:])
+        last = tile([P, C], F32, "last")
         put(3, last[:, 64 : 64 + J])
         for h in range(2):
             fetch_levels(last[:, h * HALF : (h + 1) * HALF], 3, h * HALF, (h + 1) * HALF)
@@ -165,48 +169,40 @@ def tile_picked_tokens_plain_bank_shrunk_store_plain_kernel(
         vs_gw = tile([P, N], U32, "vs_gw")
 
         halves = [slice(h * HALF, (h + 1) * HALF) for h in range(2)]
-        mags = [tile([P, C], F32, "mags%d" % t) for t in range(2)]
-        early = tile([P, 2 * C], F32, "early")
-        hid = [tile([P, HALF * PACK], BF16, "hid%d" % h) for h in range(2)]
+        mags = [tile([P, C], F32, "mags0", tag="xt_gw"), tile([P, C], F32, "mags1")]
+        diffs = tile([P, 2 * PACK * HALF], F32, "diffs")
+        diffs_by_tile = diffs[:].rearrange("p (h t c) -> p t h c", h=2, t=PACK)
+        hid = tile([P, HALF * PACK], BF16, "hid")
         codes = tile([P, C], U32, "codes")
         planes = tile([P, C], U8, "planes")
+
+        def by_half(ap):
+            return ap.rearrange("p (h c) -> p h c", h=2)
 
         def magnitude(t, cs):
             nc.vector.scalar_tensor_tensor(
                 out=mags[t][:, cs], in0=boards[t][:, cs], scalar=-1.0, in1=boards[t][:, cs], op0=ALU.mult, op1=ALU.max
             )
 
-        def take_off(dst, t, cs):
-            nc.vector.tensor_tensor(dst, mags[t][:, cs], cut[t][:, cs], ALU.subtract)
-
-        def keep_positive(h, t0, pair):
-            nc.vector.tensor_scalar(
-                out=hid[h][:].rearrange("p (c t) -> p c t", t=PACK)[:, :, t0 : t0 + 2], in0=pair,
-                scalar1=0.0, scalar2=None, op0=ALU.max,
-            )
-
         whole = slice(0, C)
-        for t in range(2):
+        for t in range(PACK - 1):
+            if t == 2:
+                nc.vector.tensor_copy(vs_gs[:], vs_sc[:].indirect(l5[:]))
+                nc.vector.tensor_copy(vs_gw[:], vs_w[:].indirect(l5[:]))
+                mags.append(tile([P, C], F32, "mags2", tag="vs_w"))
             magnitude(t, whole)
-            take_off(early[:, t * C : (t + 1) * C], t, whole)
-        nc.vector.tensor_copy(vs_gs[:], vs_sc[:].indirect(l5[:]))
-        nc.vector.tensor_copy(vs_gw[:], vs_w[:].indirect(l5[:]))
-        for h, cs in enumerate(halves):
-            keep_positive(h, 0, early[:].rearrange("p (t c) -> p c t", t=2)[:, cs, :])
-        mags.append(tile([P, C], F32, "mags2", tag="vs_w"))
-        mags.append(mags[2])
-        late = [tile([P, 2 * HALF], F32, "late0", tag="vs_sc"), tile([P, 2 * HALF], F32, "late1")]
-        magnitude(2, whole)
-        for h, cs in enumerate(halves):
-            take_off(late[h][:, 0:HALF], 2, cs)
+            nc.vector.tensor_tensor(diffs_by_tile[:, t], by_half(mags[t][:]), by_half(cut[t]), ALU.subtract)
+        mags.append(tile([P, C], F32, "mags3", tag="vs_w"))
         for cs in halves:
             magnitude(3, cs)
-        out_rows = out.rearrange("(u p) c -> p u c", p=P)
         for h, cs in enumerate(halves):
-            take_off(late[h][:, HALF : 2 * HALF], 3, cs)
-            keep_positive(h, 2, late[h][:].rearrange("p (t c) -> p c t", t=2))
-            nc.vector.quantize_mx(out=codes[:, cs].bitcast(FP8X4), scales=planes[:, cs], in_=hid[h][:])
-            res = tile([P, N // P, HALF], F32, "res%d" % h)
+            nc.vector.tensor_tensor(diffs_by_tile[:, 3, h], mags[3][:, cs], cut[3][:, cs], ALU.subtract)
+            nc.vector.tensor_scalar(
+                out=hid[:].rearrange("p (c t) -> p c t", t=PACK),
+                in0=diffs[:, h * PACK * HALF : (h + 1) * PACK * HALF].rearrange("p (t c) -> p c t", t=PACK),
+                scalar1=0.0, scalar2=None, op0=ALU.max,
+            )
+            nc.vector.quantize_mx(out=codes[:, cs].bitcast(FP8X4), scales=planes[:, cs], in_=hid[:])
             for u in range(N // P):
                 rows = slice(u * P, (u + 1) * P)
                 y = ps.tile([P, HALF], F32, name="y%d%d" % (h, u))
@@ -214,8 +210,9 @@ def tile_picked_tokens_plain_bank_shrunk_store_plain_kernel(
                     out=y[:], lhsT=vs_gw[:, rows].bitcast(FP8X4), lhsT_scale=vs_gs[:, rows],
                     rhs=codes[:, cs].bitcast(FP8X4), rhs_scale=planes[:, cs], start=True, stop=True,
                 )
+                res = tile([P, HALF], F32, "res%d%d" % (h, u))
                 if h == 1 and u == 1:
-                    nc.vector.tensor_copy(res[:, u, :], y[:])
+                    nc.vector.tensor_copy(res[:], y[:])
                 else:
-                    nc.scalar.copy(res[:, u, :], y[:])
-            nc.sync.dma_start(out=out_rows[:, :, cs], in_=res[:])
+                    nc.scalar.copy(res[:], y[:])
+                nc.sync.dma_start(out=out[rows, cs], in_=res[:])

@@ -12,13 +12,22 @@ FP8X4 = mybir.dt.float8_e4m3fn_x4
 FP4X4 = mybir.dt.float4_e2m1fn_x4
 ALU = mybir.AluOpType
 COPY = mybir.ActivationFunctionType.Copy
+RELU = mybir.ActivationFunctionType.Relu
+
+K, J, R, T, Z, M, C, D, N, S = 512, 384, 512, 2048, 512, 1024, 512, 1024, 256, 1024
 
 P = 128
 PACK = 4
 QUADS = 4
-K, J, R, T, Z, M, C, D, N, S = 512, 384, 512, 2048, 512, 1024, 512, 1024, 256, 1024
+QUAD = P // QUADS
+SCALE_ROWS = 4
+PER_COLUMN = 16
+LINE = 4
+LAST = PACK - 1
 HALF = C // 2
-SLOT_PIECES = ((0, 256), (256, 384))
+SLOT_PIECES = ((0, 256), (256, J))
+W_QUAD = 2
+SCALAR_SHARE = HALF // 2
 
 FLOPS = 2 * K * R * J + 2 * Z * R * J + 2 * R * N * C
 
@@ -36,183 +45,201 @@ def tile_picked_tokens_plain_bank_shrunk_store_plain_kernel(
         def tile(shape, dtype, name, tag=None):
             return sb.tile(shape, dtype, name=name, tag=tag or name, align_bytes=64)
 
+        def quad_rows(q, count):
+            return slice(QUAD * q, QUAD * q + count)
+
         def load_list(src, name):
             dst = lists.tile([P, src.shape[1]], U16, name=name)
             nc.sync.dma_start(dst[:], src)
             return dst
 
-        def load_scale_rows(queue, dst, src):
+        def load_scale_rows(dst, src):
             for q in range(QUADS):
-                queue.dma_start(out=dst[32 * q : 32 * q + 4, :].bitcast(I32), in_=src[0, 4 * q : 4 * q + 4, :].bitcast(I32))
+                nc.sync.dma_start(
+                    out=dst[quad_rows(q, SCALE_ROWS), :].bitcast(I32),
+                    in_=src[0, SCALE_ROWS * q : SCALE_ROWS * (q + 1), :].bitcast(I32),
+                )
 
-        def words8(src):
-            return src[0].rearrange("p c b -> p (c b)").bitcast(I32)
+        def stage_scale_rows(dst, src):
+            nc.sync.dma_start(out=dst.bitcast(I32), in_=src[0].bitcast(I32).rearrange("(q i) c -> i q c", q=QUADS))
 
-        xo_sc = tile([P, M], U8, "xo_sc")
-        xt_sc = tile([P, T], U8, "xt_sc")
-        vs_sc = tile([P, S], U8, "vs_sc")
-        wst = tile([4, QUADS, 2 * R], U8, "wst")
-        wsc = tile([P, 2 * R], U8, "wsc")
-        xo_st = tile([4, QUADS, M], U8, "xo_st")
+        def load_words(dst, src):
+            nc.sync.dma_start(out=dst[:].bitcast(I32), in_=src.bitcast(I32))
+
+        def e4m3_bytes(src):
+            return src[0].rearrange("p c b -> p (c b)")
+
+        xo_scale_win = tile([P, M], U8, "xo_scale_win")
+        xt_scale_win = tile([P, T], U8, "xt_scale_win")
+        vs_scale_win = tile([P, S], U8, "vs_scale_win")
+        w_scale_blocks = tile([P, QUADS, 2 * R], U8, "w_scale_blocks")
+        xo_scale_stage = tile([SCALE_ROWS, QUADS, M], U8, "xo_scale_stage")
         boards = [tile([P, C], F32, "board%d" % t) for t in range(PACK)]
-        nc.vector.memset(wsc[:].bitcast(I32), 0)
-        nc.vector.memset(xo_sc[:].bitcast(I32), 0)
-        nc.vector.memset(xt_sc[:].bitcast(I32), 0)
-        nc.vector.memset(vs_sc[:].bitcast(I32), 0)
+        nc.vector.memset(w_scale_blocks[:, 0 : W_QUAD + 1, :].bitcast(I32), 0)
+        nc.vector.memset(xo_scale_win[:].bitcast(I32), 0)
+        nc.vector.memset(xt_scale_win[:].bitcast(I32), 0)
         for t in range(PACK):
             nc.vector.memset(boards[t][:], 0.0)
 
         steps = tile([P, PACK], F32, "steps")
-
-        def stage_scales(queue, dst, src):
-            queue.dma_start(
-                out=dst.bitcast(I32),
-                in_=src[0].bitcast(I32).rearrange("(q i) c -> i q c", q=QUADS),
-            )
-
         levels = [tile([P, D], F32, "levels%d" % t) for t in range(PACK)]
         tl_rows = tl.rearrange("(p t) d -> t p d", t=PACK)
-        xt_w = tile([P, T], U32, "xt_w")
-        xo_w = tile([P, M], U16, "xo_w")
-        vs_w = tile([P, S], U32, "vs_w")
-        w_w = tile([P, R], U16, "w_w")
-        w2_w = tile([P, R], U32, "w2_w")
+        xt_word_win = tile([P, T], U32, "xt_word_win")
+        xo_word_win = tile([P, M], U16, "xo_word_win")
+        vs_word_win = tile([P, S], U32, "vs_word_win")
+        w_raw = tile([P, R], U16, "w_raw")
+        w2_raw = tile([P, R], U32, "w2_raw")
 
-        nc.gpsimd.dma_start(out=w_w[:].bitcast(I32), in_=w_words[0].bitcast(I32))
         nc.gpsimd.dma_start(out=steps[:], in_=sl.rearrange("(p t) o -> p (t o)", t=PACK))
-        stage_scales(nc.sync, wst[:, :, 0:R], w_scales)
-        stage_scales(nc.sync, wst[:, :, R : 2 * R], w2_scales)
-        l2 = load_list(offs2, "l2")
-        stage_scales(nc.sync, xo_st[:], xo_scales)
-        nc.sync.dma_start(out=xo_w[:].bitcast(I32), in_=xo_words[0].bitcast(I32))
-        nc.sync.dma_start(out=w2_w[:].bitcast(I32), in_=words8(w2_words))
-        l1 = load_list(offs, "l1")
-        nc.sync.dma_start(out=xt_w[:].bitcast(I32), in_=words8(xt_words))
-        load_scale_rows(nc.sync, xt_sc, xt_scales)
-        l4 = load_list(offs4, "l4")
-        for t in range(PACK - 1):
+        nc.gpsimd.memset(vs_scale_win[:].bitcast(I32), 0)
+        stage_scale_rows(xo_scale_stage[:], xo_scales)
+        note_list = load_list(offs2, "note_list")
+        level_list = load_list(offs4, "level_list")
+        load_words(xo_word_win, xo_words[0])
+        stage_scale_rows(w_scale_blocks[quad_rows(W_QUAD, SCALE_ROWS), :, 0:R], w_scales)
+        stage_scale_rows(w_scale_blocks[quad_rows(W_QUAD, SCALE_ROWS), :, R : 2 * R], w2_scales)
+        load_words(w2_raw, e4m3_bytes(w2_words))
+        nc.sync.dma_start(out=levels[0][:], in_=tl_rows[0])
+        token_list = load_list(offs, "token_list")
+        load_scale_rows(xt_scale_win, xt_scales)
+        load_words(xt_word_win, e4m3_bytes(xt_words))
+        load_words(w_raw, w_words[0])
+        for t in range(1, LAST):
             nc.sync.dma_start(out=levels[t][:], in_=tl_rows[t])
-        l3 = load_list(offs3, "l3")
-        nc.sync.dma_start(out=levels[3][:], in_=tl_rows[3])
-        load_scale_rows(nc.sync, vs_sc, vs_scales)
-        l5 = load_list(offs5, "l5")
-        nc.sync.dma_start(out=vs_w[:].bitcast(I32), in_=words8(vs_words))
+        board_list = load_list(offs3, "board_list")
+        nc.sync.dma_start(out=levels[LAST][:], in_=tl_rows[LAST])
+        load_scale_rows(vs_scale_win, vs_scales)
+        store_list = load_list(offs5, "store_list")
+        load_words(vs_word_win, e4m3_bytes(vs_words))
 
-        cuts = [tile([P, C], F32, "cut%d" % t) for t in range(PACK - 1)]
+        cuts = [tile([P, C], F32, "cut%d" % t)[:] for t in range(LAST)]
 
-        def fetch_levels(dst, t, c0, c1):
-            nc.scalar.activation(
-                out=dst, in_=levels[t][:].indirect(l4[:, c0 // 16 : c1 // 16]), func=COPY, scale=steps[:, t : t + 1]
-            )
+        def fetch_cuts(dst, t, cols):
+            offsets = level_list[:, cols.start // PER_COLUMN : cols.stop // PER_COLUMN]
+            nc.scalar.activation(out=dst, in_=levels[t][:].indirect(offsets), func=COPY, scale=steps[:, t : t + 1])
 
-        xo_gs = tile([P, J], U8, "xo_gs")
-        xo_gw = tile([P, J], U16, "xo_gw")
-        xt_gs = tile([P, J], U8, "xt_gs")
-        xt_gw = tile([P, J], U32, "xt_gw")
-        wds = tile([P, 2, R], U8, "wds")
-        w2_dw = tile([P, R], U32, "w2_dw")
-
-        def dealt(ap):
-            return ap.rearrange("p (t m) -> p t m", t=PACK)
-
-        def undealt(ap):
-            return ap.rearrange("p (m t) -> p t m", t=PACK)
-
-        for q in range(QUADS):
-            nc.vector.tensor_copy(wsc[32 * q : 32 * q + 4, :].bitcast(I32), wst[:, q, :].bitcast(I32))
-        for q in range(QUADS):
-            nc.vector.tensor_copy(xo_sc[32 * q : 32 * q + 4, :].bitcast(I32), xo_st[:, q, :].bitcast(I32))
-        nc.gpsimd.tensor_copy(dealt(wds[:, 1, :]), undealt(wsc[:, R : 2 * R]))
-        nc.gpsimd.tensor_copy(dealt(wds[:, 0, :]), undealt(wsc[:, 0:R]))
-        nc.scalar.copy(dealt(w2_dw[:]), undealt(w2_w[:]))
-        w_dw = tile([P, R], U16, "w_dw", tag="w2_w")
-        nc.scalar.copy(dealt(w_dw[:]), undealt(w_w[:]))
-        nc.vector.tensor_copy(xo_gs[:], xo_sc[:].indirect(l2[:]))
-        nc.vector.tensor_copy(xo_gw[:], xo_w[:].indirect(l2[:]))
-        nc.vector.tensor_copy(xt_gw[:], xt_w[:].indirect(l1[:]))
-        nc.vector.tensor_copy(xt_gs[:], xt_sc[:].indirect(l1[:]))
-
-        accs = [ps.tile([P, C], F32, name="acc%d" % t) for t in range(PACK)]
-        for t in range(PACK):
-            cols = slice(t * P, (t + 1) * P)
-            for i, (j0, j1) in enumerate(SLOT_PIECES):
-                nc.tensor.matmul_mx(
-                    out=accs[t][:, j0:j1], lhsT=w2_dw[:, cols].bitcast(FP8X4), lhsT_scale=wds[:, 1, cols],
-                    rhs=xo_gw[:, j0:j1].bitcast(FP4X4), rhs_scale=xo_gs[:, j0:j1], start=(i == 0), stop=False,
-                )
-        for t in range(PACK):
-            cols = slice(t * P, (t + 1) * P)
-            for i, (j0, j1) in enumerate(SLOT_PIECES):
-                nc.tensor.matmul_mx(
-                    out=accs[t][:, j0:j1], lhsT=w_dw[:, cols].bitcast(FP4X4), lhsT_scale=wds[:, 0, cols],
-                    rhs=xt_gw[:, j0:j1].bitcast(FP8X4), rhs_scale=xt_gs[:, j0:j1],
-                    start=False, stop=(i == len(SLOT_PIECES) - 1),
-                )
-
-        def put(t, src):
-            nc.vector.tensor_copy(src, accs[t][:, 0:J])
-            nc.scalar.activation(out=boards[t][:].indirect(l3[:]), in_=src, func=COPY)
-
-        fetch_levels(cuts[0][:], 0, 0, C)
-        fetch_levels(cuts[1][:], 1, 0, C)
-        fetch_levels(cuts[2][:], 2, 0, C)
-        put(0, tile([P, J], F32, "hidden0")[:])
-        put(1, tile([P, J], F32, "hidden1")[:])
-        put(2, tile([P, J], F32, "hidden2")[:])
-        last = tile([P, C], F32, "last")
-        put(3, last[:, 64 : 64 + J])
-        for h in range(2):
-            fetch_levels(last[:, h * HALF : (h + 1) * HALF], 3, h * HALF, (h + 1) * HALF)
-        cut = [c[:] for c in cuts] + [last[:]]
-
-        vs_gs = tile([P, N], U8, "vs_gs")
-        vs_gw = tile([P, N], U32, "vs_gw")
-
+        whole = slice(0, C)
         halves = [slice(h * HALF, (h + 1) * HALF) for h in range(2)]
-        mags = [tile([P, C], F32, "mags0", tag="xt_gw"), tile([P, C], F32, "mags1")]
+
+        xo_scale_got = tile([P, J], U8, "xo_scale_got")
+        xo_word_got = tile([P, J], U16, "xo_word_got")
+        xt_scale_got = tile([P, J], U8, "xt_scale_got")
+        xt_word_got = tile([P, J], U32, "xt_word_got")
+        w_scale_dealt = tile([P, 2, R], U8, "w_scale_dealt")
+        w2_dealt = tile([P, R], U32, "w2_dealt")
+
+        def deal_words(dst, src):
+            nc.scalar.copy(dst[:].rearrange("p (t m) -> p t m", t=PACK), src[:].rearrange("p (m t) -> p t m", t=PACK))
+
+        for q in range(QUADS):
+            nc.vector.tensor_copy(
+                xo_scale_win[quad_rows(q, SCALE_ROWS), :].bitcast(I32), xo_scale_stage[:, q, :].bitcast(I32)
+            )
+        nc.vector.tensor_copy(xo_scale_got[:], xo_scale_win[:].indirect(note_list[:]))
+        for q in range(QUADS):
+            if q != W_QUAD:
+                count = QUAD if q < W_QUAD else SCALE_ROWS
+                nc.vector.tensor_copy(
+                    w_scale_blocks[quad_rows(q, count), W_QUAD, :].bitcast(I32),
+                    w_scale_blocks[quad_rows(W_QUAD, count), q, :].bitcast(I32),
+                )
+        nc.vector.tensor_copy(xo_word_got[:], xo_word_win[:].indirect(note_list[:]))
+        nc.vector.tensor_copy(
+            w_scale_dealt[:].rearrange("p w (t m) -> p w t m", t=PACK),
+            w_scale_blocks[:, W_QUAD, :].rearrange("p (w m t) -> p w t m", w=2, t=PACK),
+        )
+        deal_words(w2_dealt, w2_raw)
+        fetch_cuts(cuts[0], 0, whole)
+        w_dealt = tile([P, R], U16, "w_dealt", tag="w2_raw")
+        deal_words(w_dealt, w_raw)
+        nc.vector.tensor_copy(xt_scale_got[:], xt_scale_win[:].indirect(token_list[:]))
+        nc.vector.tensor_copy(xt_word_got[:], xt_word_win[:].indirect(token_list[:]))
+
+        sums = [ps.tile([P, C], F32, name="sum%d" % t) for t in range(PACK)]
+        for t in range(PACK):
+            cols = slice(t * P, (t + 1) * P)
+            for j0, j1 in SLOT_PIECES:
+                nc.tensor.matmul_mx(
+                    out=sums[t][:, j0:j1], lhsT=w2_dealt[:, cols].bitcast(FP8X4), lhsT_scale=w_scale_dealt[:, 1, cols],
+                    rhs=xo_word_got[:, j0:j1].bitcast(FP4X4), rhs_scale=xo_scale_got[:, j0:j1],
+                    start=(j0 == 0), stop=False,
+                )
+        for t in range(PACK):
+            cols = slice(t * P, (t + 1) * P)
+            for j0, j1 in SLOT_PIECES:
+                nc.tensor.matmul_mx(
+                    out=sums[t][:, j0:j1], lhsT=w_dealt[:, cols].bitcast(FP4X4), lhsT_scale=w_scale_dealt[:, 0, cols],
+                    rhs=xt_word_got[:, j0:j1].bitcast(FP8X4), rhs_scale=xt_scale_got[:, j0:j1],
+                    start=False, stop=(j1 == J),
+                )
+
+        def put_on_board(t, hidden):
+            nc.vector.tensor_copy(hidden, sums[t][:, 0:J])
+            nc.scalar.activation(out=boards[t][:].indirect(board_list[:]), in_=hidden, func=COPY)
+
+        for t in range(1, LAST):
+            fetch_cuts(cuts[t], t, whole)
+        for t in range(LAST):
+            put_on_board(t, tile([P, J], F32, "hidden%d" % t)[:])
+        last_cut = tile([P, C], F32, "last_cut")
+        put_on_board(LAST, last_cut[:, (C - J) // 2 : (C + J) // 2])
+        for cols in halves:
+            fetch_cuts(last_cut[:, cols], LAST, cols)
+        cuts.append(last_cut[:])
+
+        vs_scale_got = tile([P, N], U8, "vs_scale_got")
+        vs_word_got = tile([P, N], U32, "vs_word_got")
+        mags = [tile([P, C], F32, "mags0", tag="xt_word_got"), tile([P, C], F32, "mags1")]
         diffs = tile([P, 2 * PACK * HALF], F32, "diffs")
         diffs_by_tile = diffs[:].rearrange("p (h t c) -> p t h c", h=2, t=PACK)
-        hid = tile([P, HALF * PACK], BF16, "hid")
-        codes = tile([P, C], U32, "codes")
-        planes = tile([P, C], U8, "planes")
+        hid = [tile([P, HALF * PACK], BF16, "hid%d" % h) for h in range(2)]
+        hid_codes = tile([P, C], U32, "hid_codes")
+        hid_scales = tile([P, C], U8, "hid_scales")
 
         def by_half(ap):
             return ap.rearrange("p (h c) -> p h c", h=2)
 
-        def magnitude(t, cs):
+        def magnitude(t, cols):
             nc.vector.scalar_tensor_tensor(
-                out=mags[t][:, cs], in0=boards[t][:, cs], scalar=-1.0, in1=boards[t][:, cs], op0=ALU.mult, op1=ALU.max
+                out=mags[t][:, cols], in0=boards[t][:, cols], scalar=-1.0, in1=boards[t][:, cols],
+                op0=ALU.mult, op1=ALU.max,
             )
 
-        whole = slice(0, C)
-        for t in range(PACK - 1):
-            if t == 2:
-                nc.vector.tensor_copy(vs_gs[:], vs_sc[:].indirect(l5[:]))
-                nc.vector.tensor_copy(vs_gw[:], vs_w[:].indirect(l5[:]))
-                mags.append(tile([P, C], F32, "mags2", tag="vs_w"))
+        def take_cuts_off(t):
             magnitude(t, whole)
-            nc.vector.tensor_tensor(diffs_by_tile[:, t], by_half(mags[t][:]), by_half(cut[t]), ALU.subtract)
-        mags.append(tile([P, C], F32, "mags3", tag="vs_w"))
-        for cs in halves:
-            magnitude(3, cs)
-        for h, cs in enumerate(halves):
-            nc.vector.tensor_tensor(diffs_by_tile[:, 3, h], mags[3][:, cs], cut[3][:, cs], ALU.subtract)
+            nc.vector.tensor_tensor(diffs_by_tile[:, t], by_half(mags[t][:]), by_half(cuts[t]), ALU.subtract)
+
+        take_cuts_off(0)
+        take_cuts_off(1)
+        nc.vector.tensor_copy(vs_scale_got[:], vs_scale_win[:].indirect(store_list[:]))
+        nc.vector.tensor_copy(vs_word_got[:], vs_word_win[:].indirect(store_list[:]))
+        mags.append(tile([P, C], F32, "mags2", tag="vs_word_win"))
+        take_cuts_off(2)
+        mags.append(tile([P, C], F32, "mags3", tag="vs_word_win"))
+        for cols in halves:
+            magnitude(LAST, cols)
+
+        for h, cols in enumerate(halves):
+            nc.vector.tensor_tensor(diffs_by_tile[:, LAST, h], mags[LAST][:, cols], cuts[LAST][:, cols], ALU.subtract)
+            woven = hid[h][:].rearrange("p (c i t) -> p c t i", i=LINE, t=PACK)
+            planar = diffs[:, h * PACK * HALF : (h + 1) * PACK * HALF].rearrange("p (t c i) -> p c t i", t=PACK, i=LINE)
+            scalar_lines = SCALAR_SHARE // LINE if h == 1 else 0
+            if scalar_lines:
+                nc.scalar.activation(out=woven[:, :scalar_lines], in_=planar[:, :scalar_lines], func=RELU)
             nc.vector.tensor_scalar(
-                out=hid[:].rearrange("p (c t) -> p c t", t=PACK),
-                in0=diffs[:, h * PACK * HALF : (h + 1) * PACK * HALF].rearrange("p (t c) -> p c t", t=PACK),
-                scalar1=0.0, scalar2=None, op0=ALU.max,
+                out=woven[:, scalar_lines:], in0=planar[:, scalar_lines:], scalar1=0.0, scalar2=None, op0=ALU.max
             )
-            nc.vector.quantize_mx(out=codes[:, cs].bitcast(FP8X4), scales=planes[:, cs], in_=hid[:])
+            nc.vector.quantize_mx(out=hid_codes[:, cols].bitcast(FP8X4), scales=hid_scales[:, cols], in_=hid[h][:])
             for u in range(N // P):
                 rows = slice(u * P, (u + 1) * P)
-                y = ps.tile([P, HALF], F32, name="y%d%d" % (h, u))
+                product = ps.tile([P, HALF], F32, name="product%d%d" % (h, u))
                 nc.tensor.matmul_mx(
-                    out=y[:], lhsT=vs_gw[:, rows].bitcast(FP8X4), lhsT_scale=vs_gs[:, rows],
-                    rhs=codes[:, cs].bitcast(FP8X4), rhs_scale=planes[:, cs], start=True, stop=True,
+                    out=product[:], lhsT=vs_word_got[:, rows].bitcast(FP8X4), lhsT_scale=vs_scale_got[:, rows],
+                    rhs=hid_codes[:, cols].bitcast(FP8X4), rhs_scale=hid_scales[:, cols], start=True, stop=True,
                 )
-                res = tile([P, HALF], F32, "res%d%d" % (h, u))
-                if h == 1 and u == 1:
-                    nc.vector.tensor_copy(res[:], y[:])
+                result = tile([P, HALF], F32, "result%d%d" % (h, u))
+                if h == 1 and u == N // P - 1:
+                    nc.vector.tensor_copy(result[:], product[:])
                 else:
-                    nc.scalar.copy(res[:], y[:])
-                nc.sync.dma_start(out=out[rows, cs], in_=res[:])
+                    nc.scalar.copy(result[:], product[:])
+                nc.sync.dma_start(out=out[rows, cols], in_=result[:])

from contextlib import ExitStack

import concourse.mybir as mybir

F32 = mybir.dt.float32
BF16 = mybir.dt.bfloat16
I32 = mybir.dt.int32
U32 = mybir.dt.uint32
U16 = mybir.dt.uint16
U8 = mybir.dt.uint8
FP8X4 = mybir.dt.float8_e4m3fn_x4
FP4X4 = mybir.dt.float4_e2m1fn_x4
ALU = mybir.AluOpType
COPY = mybir.ActivationFunctionType.Copy
RELU = mybir.ActivationFunctionType.Relu

K, J, R, T, Z, M, C, D, N, S = 512, 384, 512, 2048, 512, 1024, 512, 1024, 256, 1024

P = 128
PACK = 4
QUADS = 4
QUAD = P // QUADS
SCALE_ROWS = 4
PER_COLUMN = 16
LINE = 4
LAST = PACK - 1
HALF = C // 2
SLOT_PIECES = ((0, 256), (256, J))
W_QUAD = 2
SCALAR_SHARE = HALF // 2

FLOPS = 2 * K * R * J + 2 * Z * R * J + 2 * R * N * C


def tile_picked_tokens_plain_bank_shrunk_store_plain_kernel(
    tc, xt_words, xt_scales, w_words, w_scales, xo_words, xo_scales, w2_words, w2_scales, tl, sl,
    vs_words, vs_scales, offs, offs2, offs3, offs4, offs5, out,
):
    nc = tc.nc
    with ExitStack() as ctx:
        lists = ctx.enter_context(tc.tile_pool(name="lists", bufs=1))
        sb = ctx.enter_context(tc.tile_pool(name="sb", bufs=1))
        ps = ctx.enter_context(tc.psum_pool(name="ps", bufs=1))

        def tile(shape, dtype, name, tag=None):
            return sb.tile(shape, dtype, name=name, tag=tag or name, align_bytes=64)

        def quad_rows(q, count):
            return slice(QUAD * q, QUAD * q + count)

        def load_list(src, name):
            dst = lists.tile([P, src.shape[1]], U16, name=name)
            nc.sync.dma_start(dst[:], src)
            return dst

        def load_scale_rows(dst, src):
            for q in range(QUADS):
                nc.sync.dma_start(
                    out=dst[quad_rows(q, SCALE_ROWS), :].bitcast(I32),
                    in_=src[0, SCALE_ROWS * q : SCALE_ROWS * (q + 1), :].bitcast(I32),
                )

        def stage_scale_rows(dst, src):
            nc.sync.dma_start(out=dst.bitcast(I32), in_=src[0].bitcast(I32).rearrange("(q i) c -> i q c", q=QUADS))

        def load_words(dst, src):
            nc.sync.dma_start(out=dst[:].bitcast(I32), in_=src.bitcast(I32))

        def e4m3_bytes(src):
            return src[0].rearrange("p c b -> p (c b)")

        xo_scale_win = tile([P, M], U8, "xo_scale_win")
        xt_scale_win = tile([P, T], U8, "xt_scale_win")
        vs_scale_win = tile([P, S], U8, "vs_scale_win")
        w_scale_blocks = tile([P, QUADS, 2 * R], U8, "w_scale_blocks")
        xo_scale_stage = tile([SCALE_ROWS, QUADS, M], U8, "xo_scale_stage")
        boards = [tile([P, C], F32, "board%d" % t) for t in range(PACK)]
        nc.vector.memset(w_scale_blocks[:, 0 : W_QUAD + 1, :].bitcast(I32), 0)
        nc.vector.memset(xo_scale_win[:].bitcast(I32), 0)
        nc.vector.memset(xt_scale_win[:].bitcast(I32), 0)
        for t in range(PACK):
            nc.vector.memset(boards[t][:], 0.0)

        steps = tile([P, PACK], F32, "steps")
        levels = [tile([P, D], F32, "levels%d" % t) for t in range(PACK)]
        tl_rows = tl.rearrange("(p t) d -> t p d", t=PACK)
        xt_word_win = tile([P, T], U32, "xt_word_win")
        xo_word_win = tile([P, M], U16, "xo_word_win")
        vs_word_win = tile([P, S], U32, "vs_word_win")
        w_raw = tile([P, R], U16, "w_raw")
        w2_raw = tile([P, R], U32, "w2_raw")

        nc.gpsimd.dma_start(out=steps[:], in_=sl.rearrange("(p t) o -> p (t o)", t=PACK))
        nc.gpsimd.memset(vs_scale_win[:].bitcast(I32), 0)
        stage_scale_rows(xo_scale_stage[:], xo_scales)
        note_list = load_list(offs2, "note_list")
        level_list = load_list(offs4, "level_list")
        load_words(xo_word_win, xo_words[0])
        stage_scale_rows(w_scale_blocks[quad_rows(W_QUAD, SCALE_ROWS), :, 0:R], w_scales)
        stage_scale_rows(w_scale_blocks[quad_rows(W_QUAD, SCALE_ROWS), :, R : 2 * R], w2_scales)
        load_words(w2_raw, e4m3_bytes(w2_words))
        nc.sync.dma_start(out=levels[0][:], in_=tl_rows[0])
        token_list = load_list(offs, "token_list")
        load_scale_rows(xt_scale_win, xt_scales)
        load_words(xt_word_win, e4m3_bytes(xt_words))
        load_words(w_raw, w_words[0])
        for t in range(1, LAST):
            nc.sync.dma_start(out=levels[t][:], in_=tl_rows[t])
        board_list = load_list(offs3, "board_list")
        nc.sync.dma_start(out=levels[LAST][:], in_=tl_rows[LAST])
        load_scale_rows(vs_scale_win, vs_scales)
        store_list = load_list(offs5, "store_list")
        load_words(vs_word_win, e4m3_bytes(vs_words))

        cuts = [tile([P, C], F32, "cut%d" % t)[:] for t in range(LAST)]

        def fetch_cuts(dst, t, cols):
            offsets = level_list[:, cols.start // PER_COLUMN : cols.stop // PER_COLUMN]
            nc.scalar.activation(out=dst, in_=levels[t][:].indirect(offsets), func=COPY, scale=steps[:, t : t + 1])

        whole = slice(0, C)
        halves = [slice(h * HALF, (h + 1) * HALF) for h in range(2)]

        xo_scale_got = tile([P, J], U8, "xo_scale_got")
        xo_word_got = tile([P, J], U16, "xo_word_got")
        xt_scale_got = tile([P, J], U8, "xt_scale_got")
        xt_word_got = tile([P, J], U32, "xt_word_got")
        w_scale_dealt = tile([P, 2, R], U8, "w_scale_dealt")
        w2_dealt = tile([P, R], U32, "w2_dealt")

        def deal_words(dst, src):
            nc.scalar.copy(dst[:].rearrange("p (t m) -> p t m", t=PACK), src[:].rearrange("p (m t) -> p t m", t=PACK))

        for q in range(QUADS):
            nc.vector.tensor_copy(
                xo_scale_win[quad_rows(q, SCALE_ROWS), :].bitcast(I32), xo_scale_stage[:, q, :].bitcast(I32)
            )
        nc.vector.tensor_copy(xo_scale_got[:], xo_scale_win[:].indirect(note_list[:]))
        for q in range(QUADS):
            if q != W_QUAD:
                count = QUAD if q < W_QUAD else SCALE_ROWS
                nc.vector.tensor_copy(
                    w_scale_blocks[quad_rows(q, count), W_QUAD, :].bitcast(I32),
                    w_scale_blocks[quad_rows(W_QUAD, count), q, :].bitcast(I32),
                )
        nc.vector.tensor_copy(xo_word_got[:], xo_word_win[:].indirect(note_list[:]))
        nc.vector.tensor_copy(
            w_scale_dealt[:].rearrange("p w (t m) -> p w t m", t=PACK),
            w_scale_blocks[:, W_QUAD, :].rearrange("p (w m t) -> p w t m", w=2, t=PACK),
        )
        deal_words(w2_dealt, w2_raw)
        fetch_cuts(cuts[0], 0, whole)
        w_dealt = tile([P, R], U16, "w_dealt", tag="w2_raw")
        deal_words(w_dealt, w_raw)
        nc.vector.tensor_copy(xt_scale_got[:], xt_scale_win[:].indirect(token_list[:]))
        nc.vector.tensor_copy(xt_word_got[:], xt_word_win[:].indirect(token_list[:]))

        sums = [ps.tile([P, C], F32, name="sum%d" % t) for t in range(PACK)]
        for t in range(PACK):
            cols = slice(t * P, (t + 1) * P)
            for j0, j1 in SLOT_PIECES:
                nc.tensor.matmul_mx(
                    out=sums[t][:, j0:j1], lhsT=w2_dealt[:, cols].bitcast(FP8X4), lhsT_scale=w_scale_dealt[:, 1, cols],
                    rhs=xo_word_got[:, j0:j1].bitcast(FP4X4), rhs_scale=xo_scale_got[:, j0:j1],
                    start=(j0 == 0), stop=False,
                )
        for t in range(PACK):
            cols = slice(t * P, (t + 1) * P)
            for j0, j1 in SLOT_PIECES:
                nc.tensor.matmul_mx(
                    out=sums[t][:, j0:j1], lhsT=w_dealt[:, cols].bitcast(FP4X4), lhsT_scale=w_scale_dealt[:, 0, cols],
                    rhs=xt_word_got[:, j0:j1].bitcast(FP8X4), rhs_scale=xt_scale_got[:, j0:j1],
                    start=False, stop=(j1 == J),
                )

        def put_on_board(t, hidden):
            nc.vector.tensor_copy(hidden, sums[t][:, 0:J])
            nc.scalar.activation(out=boards[t][:].indirect(board_list[:]), in_=hidden, func=COPY)

        for t in range(1, LAST):
            fetch_cuts(cuts[t], t, whole)
        for t in range(LAST):
            put_on_board(t, tile([P, J], F32, "hidden%d" % t)[:])
        last_cut = tile([P, C], F32, "last_cut")
        put_on_board(LAST, last_cut[:, (C - J) // 2 : (C + J) // 2])
        for cols in halves:
            fetch_cuts(last_cut[:, cols], LAST, cols)
        cuts.append(last_cut[:])

        vs_scale_got = tile([P, N], U8, "vs_scale_got")
        vs_word_got = tile([P, N], U32, "vs_word_got")
        mags = [tile([P, C], F32, "mags0", tag="xt_word_got"), tile([P, C], F32, "mags1")]
        diffs = tile([P, 2 * PACK * HALF], F32, "diffs")
        diffs_by_tile = diffs[:].rearrange("p (h t c) -> p t h c", h=2, t=PACK)
        hid = [tile([P, HALF * PACK], BF16, "hid%d" % h) for h in range(2)]
        hid_codes = tile([P, C], U32, "hid_codes")
        hid_scales = tile([P, C], U8, "hid_scales")

        def by_half(ap):
            return ap.rearrange("p (h c) -> p h c", h=2)

        def magnitude(t, cols):
            nc.vector.scalar_tensor_tensor(
                out=mags[t][:, cols], in0=boards[t][:, cols], scalar=-1.0, in1=boards[t][:, cols],
                op0=ALU.mult, op1=ALU.max,
            )

        def take_cuts_off(t):
            magnitude(t, whole)
            nc.vector.tensor_tensor(diffs_by_tile[:, t], by_half(mags[t][:]), by_half(cuts[t]), ALU.subtract)

        take_cuts_off(0)
        take_cuts_off(1)
        nc.vector.tensor_copy(vs_scale_got[:], vs_scale_win[:].indirect(store_list[:]))
        nc.vector.tensor_copy(vs_word_got[:], vs_word_win[:].indirect(store_list[:]))
        mags.append(tile([P, C], F32, "mags2", tag="vs_word_win"))
        take_cuts_off(2)
        mags.append(tile([P, C], F32, "mags3", tag="vs_word_win"))
        for cols in halves:
            magnitude(LAST, cols)

        for h, cols in enumerate(halves):
            nc.vector.tensor_tensor(diffs_by_tile[:, LAST, h], mags[LAST][:, cols], cuts[LAST][:, cols], ALU.subtract)
            woven = hid[h][:].rearrange("p (c i t) -> p c t i", i=LINE, t=PACK)
            planar = diffs[:, h * PACK * HALF : (h + 1) * PACK * HALF].rearrange("p (t c i) -> p c t i", t=PACK, i=LINE)
            scalar_lines = SCALAR_SHARE // LINE if h == 1 else 0
            if scalar_lines:
                nc.scalar.activation(out=woven[:, :scalar_lines], in_=planar[:, :scalar_lines], func=RELU)
            nc.vector.tensor_scalar(
                out=woven[:, scalar_lines:], in0=planar[:, scalar_lines:], scalar1=0.0, scalar2=None, op0=ALU.max
            )
            nc.vector.quantize_mx(out=hid_codes[:, cols].bitcast(FP8X4), scales=hid_scales[:, cols], in_=hid[h][:])
            for u in range(N // P):
                rows = slice(u * P, (u + 1) * P)
                product = ps.tile([P, HALF], F32, name="product%d%d" % (h, u))
                nc.tensor.matmul_mx(
                    out=product[:], lhsT=vs_word_got[:, rows].bitcast(FP8X4), lhsT_scale=vs_scale_got[:, rows],
                    rhs=hid_codes[:, cols].bitcast(FP8X4), rhs_scale=hid_scales[:, cols], start=True, stop=True,
                )
                result = tile([P, HALF], F32, "result%d%d" % (h, u))
                if h == 1 and u == N // P - 1:
                    nc.vector.tensor_copy(result[:], product[:])
                else:
                    nc.scalar.copy(result[:], product[:])
                nc.sync.dma_start(out=out[rows, cols], in_=result[:])
